import numpy as np
import ml_dtypes


def mxq(x, axis, fmt="e4m3"):
    dtype, down = {"e4m3": (ml_dtypes.float8_e4m3fn, 7), "e5m2": (ml_dtypes.float8_e5m2, 14)}[fmt]
    v = np.moveaxis(np.asarray(x, np.float32).astype(ml_dtypes.bfloat16).astype(np.float64), axis, -1)
    blocks = v.reshape(v.shape[:-1] + (-1, 32))
    amax = np.abs(blocks).max(-1, keepdims=True)
    byte = np.maximum(np.where(amax > 0, np.frexp(amax)[1] - 1 + 127, 0) - down, 1)
    scale = np.exp2(byte - 127.0)
    codes = (blocks / scale).astype(np.float32).astype(dtype).astype(np.float64)
    return np.moveaxis((codes * scale).reshape(v.shape), -1, axis)


WIDE = False


def mx_kscale(k):
    if not WIDE:
        return np.ones(k)
    levels = np.array([24, -24, 12, -12, 0])
    if k % 512:
        return np.exp2(np.random.permutation(np.resize(levels, k // 32))).repeat(32)
    a = np.empty((k // 512, 16))
    for p in range(k // 512):
        a[p, :8] = np.random.permutation(np.resize(levels, 8))
        for g in range(8):
            far = levels[np.abs(levels - a[p, g]) >= 10]
            a[p, g + 8] = far[np.random.randint(len(far))]
    return np.exp2(a.ravel()).repeat(32)


def f64(x):
    return np.asarray(x).astype(np.float64)


def striped(idx):
    return np.tile(idx.reshape(-1, 16).T, (8, 1)).astype(np.uint16)


def unstriped(offs):
    return offs[:16].T.reshape(-1).astype(np.int64)


E2M1 = np.array([0.0, 0.5, 1.0, 1.5, 2.0, 3.0, 4.0, 6.0, -0.0, -0.5, -1.0, -1.5, -2.0, -3.0, -4.0, -6.0])


def pack_weight(w, fmt):
    k, n = w.shape
    w = f64(np.asarray(w, np.float32).astype(ml_dtypes.bfloat16)).reshape(k // 32, 32, n)
    amax = np.abs(w).max(1)
    if fmt == "e4m3":
        byte = np.frexp(amax)[1] - 1 + 127 - 7
    else:
        mant, ex = np.frexp(amax / 6.0)
        byte = np.where(mant > 0.5, ex, ex - 1) + 127
    byte = np.clip(np.where(amax > 0, byte, 1), 1, 254)
    scaled = (w * np.exp2(127.0 - byte)[:, None, :]).reshape(k, n).astype(np.float32)
    by_word = np.ascontiguousarray(scaled.reshape(k // 512, 128, 4, n).transpose(0, 1, 3, 2))
    if fmt == "e4m3":
        words = by_word.astype(ml_dtypes.float8_e4m3fn).view(np.uint8)
    else:
        c = by_word.astype(ml_dtypes.float4_e2m1fn).view(np.uint8) & 0xF
        words = (c[..., 0::2] | (c[..., 1::2] << 4)).reshape(k // 512, 128, 2 * n)
    return np.ascontiguousarray(words), np.ascontiguousarray(byte.astype(np.uint8).reshape(k // 512, 16, n))


def unpack_weight(words, scales, fmt):
    g, _, n = scales.shape
    words = np.ascontiguousarray(words).reshape(g, 128, n, -1)
    if fmt == "e4m3":
        vals = words.view(ml_dtypes.float8_e4m3fn).astype(np.float64)
    else:
        nib = np.empty((g, 128, n, 4), np.uint8)
        nib[..., 0::2] = words & 0xF
        nib[..., 1::2] = words >> 4
        vals = E2M1[nib]
    vals = vals * np.repeat(np.exp2(scales.astype(np.float64) - 127.0), 8, axis=1)[..., None]
    return vals.transpose(0, 1, 3, 2).reshape(g * 512, n)


def pack_table4(v):
    words, scales = pack_weight(v, "e2m1")
    g, t = words.shape[0] // 2, v.shape[1]
    return np.ascontiguousarray(words.reshape(g, 2, 128, t, 2).transpose(0, 2, 3, 1, 4).reshape(g, 128, t, 4)), scales


def unpack_table4(words, scales):
    g, _, t, _ = words.shape
    return unpack_weight(words.reshape(g, 128, t, 2, 2).transpose(0, 3, 1, 2, 4).reshape(2 * g, 128, 2 * t), scales, "e2m1")


K, R, M, T, N, J = 512, 1024, 512, 4096, 512, 1024


def setup_inputs():
    n = np.random.standard_normal
    u = mx_kscale(R)[:, None]
    s = mx_kscale(K)[:, None]
    p_w4 = pack_weight(n((K, R)) / np.sqrt(K) / s / u.T, "e2m1")
    p_tab = pack_table4(n((R, T)) * u)
    return {
        "x": (n((K, M)) * s).astype(np.float32),
        "w4_words": p_w4[0],
        "w4_scales": p_w4[1],
        "tab_words": p_tab[0],
        "tab_scales": p_tab[1],
        "wv": (n((R, N)) / np.sqrt(R) / u).astype(np.float32),
        "offs": striped(np.random.permutation(T)[:J]),
    }


def reference(x, w4_words, w4_scales, tab_words, tab_scales, wv, offs):
    idx = unstriped(offs)
    x_ = mxq(f64(x), 0, "e4m3")
    w4_ = unpack_weight(w4_words, w4_scales, "e2m1")
    qa = w4_.T @ x_
    qa_ = mxq(qa, 0, "e4m3")
    tab_ = unpack_table4(tab_words, tab_scales)[:, idx]
    sc = qa_.T @ tab_
    wv_ = mxq(f64(wv), 0, "e4m3")
    vv = wv_.T @ tab_
    return 8.0 * np.tanh(sc * 0.00390625), vv

@@ -1,0 +1,205 @@
+from contextlib import ExitStack
+
+import concourse.mybir as mybir
+
+K, R, M, T, N, J = 512, 1024, 512, 4096, 512, 1024
+FLOPS = 2 * K * R * M + 2 * R * M * J + 2 * R * N * J
+
+F32 = mybir.dt.float32
+BF16 = mybir.dt.bfloat16
+I32 = mybir.dt.int32
+U32 = mybir.dt.uint32
+U16 = mybir.dt.uint16
+U8 = mybir.dt.uint8
+FP8X4 = mybir.dt.float8_e4m3fn_x4
+FP4X4 = mybir.dt.float4_e2m1fn_x4
+TANH = mybir.ActivationFunctionType.Tanh
+MULT = mybir.AluOpType.mult
+
+P = 128
+PACK = 4
+PASSES = R // (P * PACK)
+BANK = 512
+HALF = 256
+
+
+def tile_list_mlat_cap_kernel(
+    tc, x, w4_words, w4_scales, tab_words, tab_scales, wv, offs, out_0, out_1
+):
+    nc = tc.nc
+    with ExitStack() as ctx:
+        keep = ctx.enter_context(tc.tile_pool(name="keep", bufs=1))
+        psum = ctx.enter_context(tc.psum_pool(name="psum", bufs=4))
+
+        def sb(name, shape, dtype, tag=None):
+            return keep.tile(shape, dtype, name=name, tag=tag or name, align_bytes=64)
+
+        offsets = keep.tile([P, J // 16], U16, name="offsets")
+        w4_raw = sb("w4_raw", [P, 2 * R], U8)
+        w4s_raw = sb("w4s_raw", [P, R], U8)
+        x_raw = sb("x_raw", [P, PACK, M], F32)
+        tab_win = sb("tab_win", [P, T], U32)
+        ts_win = sb("ts_win", [P, T], U8)
+        wv_raw = sb("wv_raw", [P, PASSES, PACK * N], F32)
+        ts_plane = sb("ts_plane", [P, PASSES * J], U8)
+        zero = sb("zero", [P, 1], F32)
+        bias = sb("bias", [P, 1], F32)
+
+        nc.vector.memset(w4s_raw[:].bitcast(I32), 0)
+        nc.vector.memset(zero[:], 0.0)
+        nc.vector.memset(ts_win[32:64, :].bitcast(I32), 0)
+        nc.vector.memset(ts_win[64:P, :].bitcast(I32), 0)
+        nc.vector.memset(ts_plane[:].bitcast(I32), 0)
+
+        nc.sync.dma_start(offsets[:], offs)
+        nc.sync.dma_start(
+            out=ts_win[0:32, :].bitcast(I32),
+            in_=tab_scales.rearrange("a q t -> q a t").bitcast(I32),
+        )
+        nc.sync.dma_start(out=w4_raw[:].bitcast(I32), in_=w4_words[0].bitcast(I32))
+        for quad in range(4):
+            nc.sync.dma_start(
+                out=w4s_raw[32 * quad : 32 * quad + 4, :].bitcast(I32),
+                in_=w4_scales[0, 4 * quad : 4 * quad + 4, :].bitcast(I32),
+            )
+        nc.sync.dma_start(out=x_raw[:], in_=x.rearrange("(p j) m -> p j m", j=PACK))
+        nc.sync.dma_start(
+            out=tab_win[:].bitcast(I32), in_=tab_words[0].rearrange("p t b -> p (t b)").bitcast(I32)
+        )
+        nc.scalar.activation(bias[:], zero[:], TANH)
+
+        ts_got = sb("ts_got", [P, J], U8)
+        nc.vector.tensor_copy(ts_got[:], ts_win[:].indirect(offsets[:]))
+        for quad in range(4):
+            nc.sync.dma_start(
+                out=ts_plane[32 * quad : 32 * quad + 4, :].bitcast(I32).rearrange("r (a w) -> r a w", a=PASSES),
+                in_=ts_got[8 * quad : 8 * quad + 8, :].bitcast(I32),
+            )
+        nc.sync.dma_start(out=wv_raw[:], in_=wv.rearrange("(a p j) n -> p a (j n)", p=P, j=PACK))
+
+        w4_ord = sb("w4_ord", [P, 2 * R], U8)
+        w4s_ord = sb("w4s_ord", [P, R], U8)
+        nc.vector.tensor_copy(
+            out=w4_ord[:].bitcast(U16).rearrange("p (b t c i) -> p b c t i", b=PASSES, t=PACK, i=8),
+            in_=w4_raw[:].bitcast(U16).rearrange("p (b c i t) -> p b c t i", b=PASSES, t=PACK, i=8),
+        )
+        nc.vector.tensor_copy(
+            out=w4s_ord[:].rearrange("p (b t c i) -> p b c t i", b=PASSES, t=PACK, i=16),
+            in_=w4s_raw[:].rearrange("p (b c i t) -> p b c t i", b=PASSES, t=PACK, i=16),
+        )
+
+        def weave(copy, dst, src):
+            copy(
+                out=dst.rearrange("p (c i t) -> p c t i", t=PACK, i=4),
+                in_=src.rearrange("p t (c i) -> p c t i", i=4),
+            )
+
+        x_codes, x_scales = [], []
+        for mt in range(M // P):
+            x_bf = sb("x_bf%d" % mt, [P, PACK * P], BF16)
+            weave(nc.scalar.copy, x_bf[:], x_raw[:, :, mt * P : (mt + 1) * P])
+            x_codes.append(sb("x_codes%d" % mt, [P, P], U32))
+            x_scales.append(sb("x_scales%d" % mt, [P, P], U8))
+            nc.vector.quantize_mx(out=x_codes[mt][:].bitcast(FP8X4), scales=x_scales[mt][:], in_=x_bf[:])
+
+        qa_bf = [sb("qa_bf0", [P, 2 * BANK], BF16), sb("qa_bf1", [P, 2 * BANK], BF16), sb("qa_bf23", [P, 4 * BANK], BF16)]
+        qa_codes, qa_scales = [], []
+
+        def quantise_qa(group, tag):
+            width = qa_bf[group].shape[1] // PACK
+            codes = sb("qa_codes%d" % group, [P, width], U32, tag)
+            scales = sb("qa_scales%d" % group, [P, width], U8)
+            nc.vector.quantize_mx(out=codes[:].bitcast(FP8X4), scales=scales[:], in_=qa_bf[group][:])
+            for c0 in range(0, width, P):
+                qa_codes.append(codes[:, c0 : c0 + P])
+                qa_scales.append(scales[:, c0 : c0 + P])
+
+        for mt in range(M // P):
+            for b in range(PASSES):
+                bank = psum.tile([P, BANK], F32, name="bank_a")
+                for t in range(PACK):
+                    c0 = (b * PACK + t) * P
+                    nc.tensor.matmul_mx(
+                        out=bank[:, t * P : (t + 1) * P],
+                        lhsT=w4_ord[:, 2 * c0 : 2 * (c0 + P)].bitcast(FP4X4),
+                        lhsT_scale=w4s_ord[:, c0 : c0 + P],
+                        rhs=x_codes[mt][:].bitcast(FP8X4),
+                        rhs_scale=x_scales[mt][:],
+                        start=True,
+                        stop=True,
+                    )
+                on_vector = b == 1 and mt < 2
+                c0 = (max(mt - 2, 0) * PASSES + b) * BANK
+                (nc.vector.tensor_copy if on_vector else nc.scalar.copy)(
+                    out=qa_bf[min(mt, 2)][:, c0 : c0 + BANK].rearrange("p (m t) -> p m t", t=PACK),
+                    in_=bank[:].rearrange("p (t m) -> p m t", t=PACK),
+                )
+            if mt < 2:
+                quantise_qa(mt, "qa_codes%d" % mt)
+
+        tab_parts = []
+        for jh in range(J // BANK):
+            got = sb("tab_got%d" % jh, [P, BANK], U32, ("qa_bf1", "qa_bf23")[jh])
+            nc.vector.tensor_copy(got[:], tab_win[:].indirect(offsets[:, jh * 32 : (jh + 1) * 32]))
+            parts = sb("tab_parts%d" % jh, [P, PASSES * 2 * BANK], U8)
+            nc.vector.tensor_copy(
+                out=parts[:].bitcast(U16).rearrange("p (d c i) -> p c d i", d=PASSES, i=8),
+                in_=got[:].bitcast(U16).rearrange("p (c i d) -> p c d i", d=PASSES, i=8),
+            )
+            tab_parts.append(parts)
+            if jh == 0:
+                quantise_qa(2, "qa_bf1")
+
+        def product(bank, codes, scales, jh):
+            for a in range(PASSES):
+                nc.tensor.matmul_mx(
+                    out=bank[:],
+                    lhsT=codes[a].bitcast(FP8X4),
+                    lhsT_scale=scales[a],
+                    rhs=tab_parts[jh][:, a * 2 * BANK : (a + 1) * 2 * BANK].bitcast(FP4X4),
+                    rhs_scale=ts_plane[:, a * J + jh * BANK : a * J + (jh + 1) * BANK],
+                    start=(a == 0),
+                    stop=(a == PASSES - 1),
+                )
+
+        for jh in range(J // BANK):
+            for mt in range(M // P):
+                bank = psum.tile([P, BANK], F32, name="bank_b")
+                product(
+                    bank,
+                    qa_codes[mt * PASSES : (mt + 1) * PASSES],
+                    qa_scales[mt * PASSES : (mt + 1) * PASSES],
+                    jh,
+                )
+                capped = sb("capped%d_%d" % (jh, mt), [P, BANK], F32)
+                nc.scalar.activation(capped[:], bank[:], TANH, bias=bias[:], scale=0.00390625)
+                score = sb("score%d_%d" % (jh, mt), [P, BANK], F32)
+                if jh == 1 and mt >= 2:
+                    nc.scalar.mul(score[:], capped[:], 8.0)
+                else:
+                    nc.vector.tensor_scalar(score[:], capped[:], 8.0, None, MULT)
+                nc.sync.dma_start(out=out_0[mt * P : (mt + 1) * P, jh * BANK : (jh + 1) * BANK], in_=score[:])
+
+        for nt in range(N // P):
+            wv_bf = sb("wv_bf%d" % nt, [P, PASSES * PACK * P], BF16, ("capped0_3", "capped1_1", None, None)[nt])
+            nc.vector.tensor_copy(
+                out=wv_bf[:].rearrange("p (a c i t) -> p a c t i", a=PASSES, t=PACK, i=4),
+                in_=wv_raw[:].rearrange("p a (t n) -> p a t n", t=PACK)[:, :, :, nt * P : (nt + 1) * P].rearrange(
+                    "p a t (c i) -> p a c t i", i=4
+                ),
+            )
+            codes = sb("wv_codes%d" % nt, [P, PASSES * P], U32)
+            scales = sb("wv_scales%d" % nt, [P, PASSES * P], U8)
+            nc.vector.quantize_mx(out=codes[:].bitcast(FP8X4), scales=scales[:], in_=wv_bf[:])
+            for jh in range(J // BANK):
+                bank = psum.tile([P, BANK], F32, name="bank_a")
+                product(
+                    bank,
+                    [codes[:, a * P : (a + 1) * P] for a in range(PASSES)],
+                    [scales[:, a * P : (a + 1) * P] for a in range(PASSES)],
+                    jh,
+                )
+                value = sb("value%d_%d" % (nt, jh), [P, BANK], F32)
+                on_vector = nt == 3 and jh == 0
+                (nc.vector.tensor_copy if on_vector else nc.scalar.copy)(out=value[:], in_=bank[:])
+                nc.sync.dma_start(out=out_1[nt * P : (nt + 1) * P, jh * BANK : (jh + 1) * BANK], in_=value[:])

@@ -29,10 +29,14 @@ def tile_list_mlat_cap_kernel(
     nc = tc.nc
     with ExitStack() as ctx:
         keep = ctx.enter_context(tc.tile_pool(name="keep", bufs=1))
+        relay = ctx.enter_context(tc.tile_pool(name="relay", bufs=1))
         psum = ctx.enter_context(tc.psum_pool(name="psum", bufs=4))
 
         def sb(name, shape, dtype, tag=None):
             return keep.tile(shape, dtype, name=name, tag=tag or name, align_bytes=64)
+
+        def relayed(name, shape, dtype, offset):
+            return relay.tile(shape, dtype, name=name, offset=offset, align_bytes=64)
 
         offsets = keep.tile([P, J // 16], U16, name="offsets")
         w4_raw = sb("w4_raw", [P, 2 * R], U8)
@@ -40,20 +44,19 @@ def tile_list_mlat_cap_kernel(
         x_raw = sb("x_raw", [P, PACK, M], F32)
         tab_win = sb("tab_win", [P, T], U32)
         ts_win = sb("ts_win", [P, T], U8)
-        wv_raw = sb("wv_raw", [P, PASSES, PACK * N], F32)
+        wv_raw = [sb("wv_raw%d" % a, [P, PACK, N], F32) for a in range(PASSES)]
         ts_plane = sb("ts_plane", [P, PASSES * J], U8)
         zero = sb("zero", [P, 1], F32)
         bias = sb("bias", [P, 1], F32)
 
         nc.vector.memset(w4s_raw[:].bitcast(I32), 0)
         nc.vector.memset(zero[:], 0.0)
-        nc.vector.memset(ts_win[32:64, :].bitcast(I32), 0)
-        nc.vector.memset(ts_win[64:P, :].bitcast(I32), 0)
+        nc.vector.memset(ts_win[0:96, :].bitcast(I32), 0)
         nc.vector.memset(ts_plane[:].bitcast(I32), 0)
 
         nc.sync.dma_start(offsets[:], offs)
         nc.sync.dma_start(
-            out=ts_win[0:32, :].bitcast(I32),
+            out=ts_win[96:P, :].bitcast(I32),
             in_=tab_scales.rearrange("a q t -> q a t").bitcast(I32),
         )
         nc.sync.dma_start(out=w4_raw[:].bitcast(I32), in_=w4_words[0].bitcast(I32))
@@ -73,9 +76,12 @@ def tile_list_mlat_cap_kernel(
         for quad in range(4):
             nc.sync.dma_start(
                 out=ts_plane[32 * quad : 32 * quad + 4, :].bitcast(I32).rearrange("r (a w) -> r a w", a=PASSES),
-                in_=ts_got[8 * quad : 8 * quad + 8, :].bitcast(I32),
+                in_=ts_got[96 + 8 * quad : 96 + 8 * quad + 8, :].bitcast(I32),
             )
-        nc.sync.dma_start(out=wv_raw[:], in_=wv.rearrange("(a p j) n -> p a (j n)", p=P, j=PACK))
+        for a in range(PASSES):
+            nc.sync.dma_start(
+                out=wv_raw[a][:], in_=wv[a * P * PACK : (a + 1) * P * PACK, :].rearrange("(p j) n -> p j n", j=PACK)
+            )
 
         w4_ord = sb("w4_ord", [P, 2 * R], U8)
         w4s_ord = sb("w4s_ord", [P, R], U8)
@@ -94,27 +100,22 @@ def tile_list_mlat_cap_kernel(
                 in_=src.rearrange("p t (c i) -> p c t i", i=4),
             )
 
-        x_codes, x_scales = [], []
-        for mt in range(M // P):
-            x_bf = sb("x_bf%d" % mt, [P, PACK * P], BF16)
-            weave(nc.scalar.copy, x_bf[:], x_raw[:, :, mt * P : (mt + 1) * P])
-            x_codes.append(sb("x_codes%d" % mt, [P, P], U32))
-            x_scales.append(sb("x_scales%d" % mt, [P, P], U8))
-            nc.vector.quantize_mx(out=x_codes[mt][:].bitcast(FP8X4), scales=x_scales[mt][:], in_=x_bf[:])
+        def quantise(name, rounded, codes):
+            scales = sb(name + "_scales", [P, codes.shape[1]], U8)
+            nc.vector.quantize_mx(out=codes[:].bitcast(FP8X4), scales=scales[:], in_=rounded)
+            return [(codes[:, c0 : c0 + P], scales[:, c0 : c0 + P]) for c0 in range(0, codes.shape[1], P)]
 
-        qa_bf = [sb("qa_bf0", [P, 2 * BANK], BF16), sb("qa_bf1", [P, 2 * BANK], BF16), sb("qa_bf23", [P, 4 * BANK], BF16)]
-        qa_codes, qa_scales = [], []
+        x_mx = []
+        for group, tiles in enumerate(((0,), (1,), (2, 3))):
+            x_bf = sb("x_bf%d" % group, [P, len(tiles) * BANK], BF16)
+            for i, mt in enumerate(tiles):
+                weave(nc.scalar.copy, x_bf[:, i * BANK : (i + 1) * BANK], x_raw[:, :, mt * P : (mt + 1) * P])
+            x_mx.extend(quantise("x%d" % group, x_bf[:], sb("x_codes%d" % group, [P, len(tiles) * P], U32)))
 
-        def quantise_qa(group, tag):
-            width = qa_bf[group].shape[1] // PACK
-            codes = sb("qa_codes%d" % group, [P, width], U32, tag)
-            scales = sb("qa_scales%d" % group, [P, width], U8)
-            nc.vector.quantize_mx(out=codes[:].bitcast(FP8X4), scales=scales[:], in_=qa_bf[group][:])
-            for c0 in range(0, width, P):
-                qa_codes.append(codes[:, c0 : c0 + P])
-                qa_scales.append(scales[:, c0 : c0 + P])
+        qa_mx = []
 
-        for mt in range(M // P):
+        def project(mt):
+            qa_bf = sb("qa_bf%d" % mt, [P, PASSES * BANK], BF16)
             for b in range(PASSES):
                 bank = psum.tile([P, BANK], F32, name="bank_a")
                 for t in range(PACK):
@@ -123,83 +124,104 @@ def tile_list_mlat_cap_kernel(
                         out=bank[:, t * P : (t + 1) * P],
                         lhsT=w4_ord[:, 2 * c0 : 2 * (c0 + P)].bitcast(FP4X4),
                         lhsT_scale=w4s_ord[:, c0 : c0 + P],
-                        rhs=x_codes[mt][:].bitcast(FP8X4),
-                        rhs_scale=x_scales[mt][:],
+                        rhs=x_mx[mt][0].bitcast(FP8X4),
+                        rhs_scale=x_mx[mt][1],
                         start=True,
                         stop=True,
                     )
-                on_vector = b == 1 and mt < 2
-                c0 = (max(mt - 2, 0) * PASSES + b) * BANK
-                (nc.vector.tensor_copy if on_vector else nc.scalar.copy)(
-                    out=qa_bf[min(mt, 2)][:, c0 : c0 + BANK].rearrange("p (m t) -> p m t", t=PACK),
+                (nc.vector.tensor_copy if mt == 0 else nc.scalar.copy)(
+                    out=qa_bf[:, b * BANK : (b + 1) * BANK].rearrange("p (m t) -> p m t", t=PACK),
                     in_=bank[:].rearrange("p (t m) -> p m t", t=PACK),
                 )
-            if mt < 2:
-                quantise_qa(mt, "qa_codes%d" % mt)
+            return qa_bf
 
-        tab_parts = []
-        for jh in range(J // BANK):
-            got = sb("tab_got%d" % jh, [P, BANK], U32, ("qa_bf1", "qa_bf23")[jh])
+        def quantise_qa(mt, qa_bf):
+            qa_mx.append(quantise("qa%d" % mt, qa_bf[:], sb("qa_codes%d" % mt, [P, PASSES * P], U32)))
+
+        def gather_words(jh):
+            got = sb("tab_got%d" % jh, [P, BANK], U32, "qa_bf1")
             nc.vector.tensor_copy(got[:], tab_win[:].indirect(offsets[:, jh * 32 : (jh + 1) * 32]))
-            parts = sb("tab_parts%d" % jh, [P, PASSES * 2 * BANK], U8)
-            nc.vector.tensor_copy(
-                out=parts[:].bitcast(U16).rearrange("p (d c i) -> p c d i", d=PASSES, i=8),
-                in_=got[:].bitcast(U16).rearrange("p (c i d) -> p c d i", d=PASSES, i=8),
-            )
-            tab_parts.append(parts)
-            if jh == 0:
-                quantise_qa(2, "qa_bf1")
+            return got
 
-        def product(bank, codes, scales, jh):
+        def part_words(jh, got):
+            parts = []
             for a in range(PASSES):
+                part = sb("tab_part%d_%d" % (jh, a), [P, 2 * BANK], U8)
+                nc.vector.tensor_copy(
+                    out=part[:].bitcast(U16),
+                    in_=got[:].bitcast(U16).rearrange("p (c a) -> p a c", a=PASSES)[:, a, :],
+                )
+                parts.append(part)
+            return parts
+
+        qa_rounded = []
+        for mt in range(M // P):
+            qa_rounded.append(project(mt))
+            if mt < 2:
+                quantise_qa(mt, qa_rounded[mt])
+        tab_parts = [part_words(0, gather_words(0))]
+        quantise_qa(2, qa_rounded[2])
+        got1 = gather_words(1)
+        quantise_qa(3, qa_rounded[3])
+        tab_parts.append(part_words(1, got1))
+
+        def product(bank, operand, jh):
+            for a, (codes, scales) in enumerate(operand):
                 nc.tensor.matmul_mx(
                     out=bank[:],
-                    lhsT=codes[a].bitcast(FP8X4),
-                    lhsT_scale=scales[a],
-                    rhs=tab_parts[jh][:, a * 2 * BANK : (a + 1) * 2 * BANK].bitcast(FP4X4),
+                    lhsT=codes.bitcast(FP8X4),
+                    lhsT_scale=scales,
+                    rhs=tab_parts[jh][a][:].bitcast(FP4X4),
                     rhs_scale=ts_plane[:, a * J + jh * BANK : a * J + (jh + 1) * BANK],
                     start=(a == 0),
                     stop=(a == PASSES - 1),
                 )
 
+        def round_wv(copy, a, half, rounded):
+            weave(copy, rounded[:], wv_raw[a][:, :, half * HALF : (half + 1) * HALF])
+            return rounded
+
+        def score_tile(jh, mt):
+            bank = psum.tile([P, BANK], F32, name="bank_b")
+            product(bank, qa_mx[mt], jh)
+            if jh == 0 and mt < 2:
+                capped = wv_raw[0][:, 2 * mt : 2 * mt + 2, 0:HALF]
+            elif jh == 0 and mt == 2:
+                capped = relayed("capped0_2", [P, 2, HALF], F32, 1984)[:]
+            else:
+                capped = sb("capped%d_%d" % (jh, mt), [P, 2, HALF], F32)[:]
+            nc.scalar.activation(
+                capped, bank[:].rearrange("p (h c) -> p h c", h=2), TANH, bias=bias[:], scale=0.00390625
+            )
+            score = sb("score%d_%d" % (jh, mt), [P, BANK], F32)
+            nc.vector.tensor_scalar(score[:].rearrange("p (h c) -> p h c", h=2), capped, 8.0, None, MULT)
+            nc.sync.dma_start(out=out_0[mt * P : (mt + 1) * P, jh * BANK : (jh + 1) * BANK], in_=score[:])
+
+        def value_tiles(half, wv_mx):
+            for i in range(2):
+                nt = 2 * half + i
+                for jh in range(J // BANK):
+                    bank = psum.tile([P, BANK], F32, name="bank_a")
+                    product(bank, [wv_mx[a][i] for a in range(PASSES)], jh)
+                    value = sb("value%d_%d" % (nt, jh), [P, BANK], F32)
+                    on_vector = half == 1 and jh == 1
+                    (nc.vector.tensor_copy if on_vector else nc.scalar.copy)(out=value[:], in_=bank[:])
+                    nc.sync.dma_start(
+                        out=out_1[nt * P : (nt + 1) * P, jh * BANK : (jh + 1) * BANK], in_=value[:]
+                    )
+
+        wv_bf00 = round_wv(nc.scalar.copy, 0, 0, sb("wv_bf00", [P, PACK * HALF], BF16, "w4_ord"))
         for jh in range(J // BANK):
             for mt in range(M // P):
-                bank = psum.tile([P, BANK], F32, name="bank_b")
-                product(
-                    bank,
-                    qa_codes[mt * PASSES : (mt + 1) * PASSES],
-                    qa_scales[mt * PASSES : (mt + 1) * PASSES],
-                    jh,
-                )
-                capped = sb("capped%d_%d" % (jh, mt), [P, BANK], F32)
-                nc.scalar.activation(capped[:], bank[:], TANH, bias=bias[:], scale=0.00390625)
-                score = sb("score%d_%d" % (jh, mt), [P, BANK], F32)
-                if jh == 1 and mt >= 2:
-                    nc.scalar.mul(score[:], capped[:], 8.0)
-                else:
-                    nc.vector.tensor_scalar(score[:], capped[:], 8.0, None, MULT)
-                nc.sync.dma_start(out=out_0[mt * P : (mt + 1) * P, jh * BANK : (jh + 1) * BANK], in_=score[:])
-
-        for nt in range(N // P):
-            wv_bf = sb("wv_bf%d" % nt, [P, PASSES * PACK * P], BF16, ("capped0_3", "capped1_1", None, None)[nt])
-            nc.vector.tensor_copy(
-                out=wv_bf[:].rearrange("p (a c i t) -> p a c t i", a=PASSES, t=PACK, i=4),
-                in_=wv_raw[:].rearrange("p a (t n) -> p a t n", t=PACK)[:, :, :, nt * P : (nt + 1) * P].rearrange(
-                    "p a t (c i) -> p a c t i", i=4
-                ),
-            )
-            codes = sb("wv_codes%d" % nt, [P, PASSES * P], U32)
-            scales = sb("wv_scales%d" % nt, [P, PASSES * P], U8)
-            nc.vector.quantize_mx(out=codes[:].bitcast(FP8X4), scales=scales[:], in_=wv_bf[:])
-            for jh in range(J // BANK):
-                bank = psum.tile([P, BANK], F32, name="bank_a")
-                product(
-                    bank,
-                    [codes[:, a * P : (a + 1) * P] for a in range(PASSES)],
-                    [scales[:, a * P : (a + 1) * P] for a in range(PASSES)],
-                    jh,
-                )
-                value = sb("value%d_%d" % (nt, jh), [P, BANK], F32)
-                on_vector = nt == 3 and jh == 0
-                (nc.vector.tensor_copy if on_vector else nc.scalar.copy)(out=value[:], in_=bank[:])
-                nc.sync.dma_start(out=out_1[nt * P : (nt + 1) * P, jh * BANK : (jh + 1) * BANK], in_=value[:])
+                score_tile(jh, mt)
+        low = [quantise("wv00", wv_bf00[:], relayed("wv_codes00", [P, HALF], U32, 2048))]
+        wv_bf10 = round_wv(nc.vector.tensor_copy, 1, 0, relayed("wv_bf10", [P, PACK * HALF], BF16, 0))
+        low.append(quantise("wv10", wv_bf10[:], sb("wv_codes10", [P, HALF], U32)))
+        value_tiles(0, low)
+        wv_bf01 = round_wv(nc.vector.tensor_copy, 0, 1, relayed("wv_bf01", [P, PACK * HALF], BF16, 3968))
+        wv_bf11 = round_wv(nc.vector.tensor_copy, 1, 1, sb("wv_bf11", [P, PACK * HALF], BF16, "capped0_3"))
+        high = [
+            quantise("wv01", wv_bf01[:], sb("wv_codes01", [P, HALF], U32)),
+            quantise("wv11", wv_bf11[:], sb("wv_codes11", [P, HALF], U32)),
+        ]
+        value_tiles(1, high)

@@ -44,7 +44,12 @@ def tile_list_mlat_cap_kernel(
         x_raw = sb("x_raw", [P, PACK, M], F32)
         tab_win = sb("tab_win", [P, T], U32)
         ts_win = sb("ts_win", [P, T], U8)
-        wv_raw = [sb("wv_raw%d" % a, [P, PACK, N], F32) for a in range(PASSES)]
+        wv_raw = {
+            (0, 0): relayed("wv_raw00", [P, PACK, HALF], F32, 0),
+            (0, 1): relayed("wv_raw01", [P, PACK, HALF], F32, 4096),
+            (1, 0): sb("wv_raw10", [P, PACK, HALF], F32),
+            (1, 1): sb("wv_raw11", [P, PACK, HALF], F32),
+        }
         ts_plane = sb("ts_plane", [P, PASSES * J], U8)
         zero = sb("zero", [P, 1], F32)
         bias = sb("bias", [P, 1], F32)
@@ -78,10 +83,14 @@ def tile_list_mlat_cap_kernel(
                 out=ts_plane[32 * quad : 32 * quad + 4, :].bitcast(I32).rearrange("r (a w) -> r a w", a=PASSES),
                 in_=ts_got[96 + 8 * quad : 96 + 8 * quad + 8, :].bitcast(I32),
             )
-        for a in range(PASSES):
-            nc.sync.dma_start(
-                out=wv_raw[a][:], in_=wv[a * P * PACK : (a + 1) * P * PACK, :].rearrange("(p j) n -> p j n", j=PACK)
-            )
+        for half in range(N // HALF):
+            for a in range(PASSES):
+                nc.sync.dma_start(
+                    out=wv_raw[half, a][:],
+                    in_=wv[a * P * PACK : (a + 1) * P * PACK, half * HALF : (half + 1) * HALF].rearrange(
+                        "(p j) n -> p j n", j=PACK
+                    ),
+                )
 
         w4_ord = sb("w4_ord", [P, 2 * R], U8)
         w4s_ord = sb("w4s_ord", [P, R], U8)
@@ -114,8 +123,7 @@ def tile_list_mlat_cap_kernel(
 
         qa_mx = []
 
-        def project(mt):
-            qa_bf = sb("qa_bf%d" % mt, [P, PASSES * BANK], BF16)
+        def project(mt, qa_bf):
             for b in range(PASSES):
                 bank = psum.tile([P, BANK], F32, name="bank_a")
                 for t in range(PACK):
@@ -133,37 +141,33 @@ def tile_list_mlat_cap_kernel(
                     out=qa_bf[:, b * BANK : (b + 1) * BANK].rearrange("p (m t) -> p m t", t=PACK),
                     in_=bank[:].rearrange("p (t m) -> p m t", t=PACK),
                 )
-            return qa_bf
 
-        def quantise_qa(mt, qa_bf):
-            qa_mx.append(quantise("qa%d" % mt, qa_bf[:], sb("qa_codes%d" % mt, [P, PASSES * P], U32)))
+        def quantise_qa(pair, qa_bf):
+            tiles = quantise("qa%d" % pair, qa_bf[:], sb("qa_codes%d" % pair, [P, 2 * PASSES * P], U32))
+            qa_mx.extend([tiles[:PASSES], tiles[PASSES:]])
 
         def gather_words(jh):
-            got = sb("tab_got%d" % jh, [P, BANK], U32, "qa_bf1")
+            got = sb("tab_got%d" % jh, [P, BANK], U32, "tab_got")
             nc.vector.tensor_copy(got[:], tab_win[:].indirect(offsets[:, jh * 32 : (jh + 1) * 32]))
             return got
 
-        def part_words(jh, got):
-            parts = []
-            for a in range(PASSES):
-                part = sb("tab_part%d_%d" % (jh, a), [P, 2 * BANK], U8)
-                nc.vector.tensor_copy(
-                    out=part[:].bitcast(U16),
-                    in_=got[:].bitcast(U16).rearrange("p (c a) -> p a c", a=PASSES)[:, a, :],
-                )
-                parts.append(part)
+        def part_words(jh, got, pieces):
+            parts = sb("tab_parts%d" % jh, [P, PASSES * 2 * BANK], U8)
+            dst = parts[:].bitcast(U16).rearrange("p (a c i) -> p c a i", a=PASSES, i=8)
+            src = got[:].bitcast(U16).rearrange("p (c i a) -> p c a i", a=PASSES, i=8)
+            step = PASSES // pieces
+            for a in range(0, PASSES, step):
+                nc.vector.tensor_copy(out=dst[:, :, a : a + step, :], in_=src[:, :, a : a + step, :])
             return parts
 
-        qa_rounded = []
+        qa_rounded = [sb("qa_bf%d" % pair, [P, 2 * PASSES * BANK], BF16) for pair in range(2)]
         for mt in range(M // P):
-            qa_rounded.append(project(mt))
-            if mt < 2:
-                quantise_qa(mt, qa_rounded[mt])
-        tab_parts = [part_words(0, gather_words(0))]
-        quantise_qa(2, qa_rounded[2])
-        got1 = gather_words(1)
-        quantise_qa(3, qa_rounded[3])
-        tab_parts.append(part_words(1, got1))
+            project(mt, qa_rounded[mt // 2][:, (mt % 2) * PASSES * BANK : (mt % 2 + 1) * PASSES * BANK])
+            if mt == 1:
+                quantise_qa(0, qa_rounded[0])
+        tab_parts = [part_words(0, gather_words(0), 2)]
+        quantise_qa(1, qa_rounded[1])
+        tab_parts.append(part_words(1, gather_words(1), 1))
 
         def product(bank, operand, jh):
             for a, (codes, scales) in enumerate(operand):
@@ -171,57 +175,54 @@ def tile_list_mlat_cap_kernel(
                     out=bank[:],
                     lhsT=codes.bitcast(FP8X4),
                     lhsT_scale=scales,
-                    rhs=tab_parts[jh][a][:].bitcast(FP4X4),
+                    rhs=tab_parts[jh][:, a * 2 * BANK : (a + 1) * 2 * BANK].bitcast(FP4X4),
                     rhs_scale=ts_plane[:, a * J + jh * BANK : a * J + (jh + 1) * BANK],
                     start=(a == 0),
                     stop=(a == PASSES - 1),
                 )
 
-        def round_wv(copy, a, half, rounded):
-            weave(copy, rounded[:], wv_raw[a][:, :, half * HALF : (half + 1) * HALF])
+        def round_wv(copy, half, rounded):
+            for a in range(PASSES):
+                weave(copy, rounded[:, a * PACK * HALF : (a + 1) * PACK * HALF], wv_raw[half, a][:])
             return rounded
 
-        def score_tile(jh, mt):
-            bank = psum.tile([P, BANK], F32, name="bank_b")
-            product(bank, qa_mx[mt], jh)
-            if jh == 0 and mt < 2:
-                capped = wv_raw[0][:, 2 * mt : 2 * mt + 2, 0:HALF]
-            elif jh == 0 and mt == 2:
-                capped = relayed("capped0_2", [P, 2, HALF], F32, 1984)[:]
-            else:
-                capped = sb("capped%d_%d" % (jh, mt), [P, 2, HALF], F32)[:]
-            nc.scalar.activation(
-                capped, bank[:].rearrange("p (h c) -> p h c", h=2), TANH, bias=bias[:], scale=0.00390625
+        def score_tiles(jh, mt0, capped):
+            count = capped.shape[1]
+            for i in range(count):
+                bank = psum.tile([P, BANK], F32, name="bank_b")
+                product(bank, qa_mx[mt0 + i], jh)
+                nc.scalar.activation(capped[:, i, :], bank[:], TANH, bias=bias[:], scale=0.00390625)
+            score = sb("score%d_%d" % (jh, mt0), [P, count, BANK], F32)
+            nc.vector.tensor_scalar(score[:], capped[:], 8.0, None, MULT)
+            nc.sync.dma_start(
+                out=out_0[mt0 * P : (mt0 + count) * P, jh * BANK : (jh + 1) * BANK].rearrange(
+                    "(i p) c -> p i c", p=P
+                ),
+                in_=score[:],
             )
-            score = sb("score%d_%d" % (jh, mt), [P, BANK], F32)
-            nc.vector.tensor_scalar(score[:].rearrange("p (h c) -> p h c", h=2), capped, 8.0, None, MULT)
-            nc.sync.dma_start(out=out_0[mt * P : (mt + 1) * P, jh * BANK : (jh + 1) * BANK], in_=score[:])
 
-        def value_tiles(half, wv_mx):
+        def value_tiles(half, rounded, codes):
+            wv_mx = quantise("wv%d" % half, rounded[:], codes)
             for i in range(2):
                 nt = 2 * half + i
+                value = sb("value%d" % nt, [P, J], F32)
                 for jh in range(J // BANK):
                     bank = psum.tile([P, BANK], F32, name="bank_a")
-                    product(bank, [wv_mx[a][i] for a in range(PASSES)], jh)
-                    value = sb("value%d_%d" % (nt, jh), [P, BANK], F32)
+                    product(bank, [wv_mx[2 * a + i] for a in range(PASSES)], jh)
+                    cols = slice(jh * BANK, (jh + 1) * BANK)
                     on_vector = half == 1 and jh == 1
-                    (nc.vector.tensor_copy if on_vector else nc.scalar.copy)(out=value[:], in_=bank[:])
-                    nc.sync.dma_start(
-                        out=out_1[nt * P : (nt + 1) * P, jh * BANK : (jh + 1) * BANK], in_=value[:]
-                    )
+                    (nc.vector.tensor_copy if on_vector else nc.scalar.copy)(out=value[:, cols], in_=bank[:])
+                    if nt == N // P - 1:
+                        nc.sync.dma_start(out=out_1[nt * P : (nt + 1) * P, cols], in_=value[:, cols])
+                if nt < N // P - 1:
+                    nc.sync.dma_start(out=out_1[nt * P : (nt + 1) * P, :], in_=value[:])
 
-        wv_bf00 = round_wv(nc.scalar.copy, 0, 0, sb("wv_bf00", [P, PACK * HALF], BF16, "w4_ord"))
-        for jh in range(J // BANK):
-            for mt in range(M // P):
-                score_tile(jh, mt)
-        low = [quantise("wv00", wv_bf00[:], relayed("wv_codes00", [P, HALF], U32, 2048))]
-        wv_bf10 = round_wv(nc.vector.tensor_copy, 1, 0, relayed("wv_bf10", [P, PACK * HALF], BF16, 0))
-        low.append(quantise("wv10", wv_bf10[:], sb("wv_codes10", [P, HALF], U32)))
-        value_tiles(0, low)
-        wv_bf01 = round_wv(nc.vector.tensor_copy, 0, 1, relayed("wv_bf01", [P, PACK * HALF], BF16, 3968))
-        wv_bf11 = round_wv(nc.vector.tensor_copy, 1, 1, sb("wv_bf11", [P, PACK * HALF], BF16, "capped0_3"))
-        high = [
-            quantise("wv01", wv_bf01[:], sb("wv_codes01", [P, HALF], U32)),
-            quantise("wv11", wv_bf11[:], sb("wv_codes11", [P, HALF], U32)),
-        ]
-        value_tiles(1, high)
+        wv_low = round_wv(nc.scalar.copy, 0, sb("wv_low", [P, PASSES * PACK * HALF], BF16))
+        score_tiles(0, 0, relayed("capped0_0", [P, 1, BANK], F32, 2112))
+        score_tiles(0, 1, relayed("capped0_1", [P, 1, BANK], F32, 4160))
+        score_tiles(0, 2, relayed("capped0_2", [P, 2, BANK], F32, 6208))
+        score_tiles(1, 0, sb("capped1_0", [P, 2, BANK], F32))
+        score_tiles(1, 2, sb("capped1_2", [P, 2, BANK], F32))
+        value_tiles(0, wv_low, relayed("wv_codes0", [P, PASSES * HALF], U32, 8256))
+        wv_high = round_wv(nc.vector.tensor_copy, 1, sb("wv_high", [P, PASSES * PACK * HALF], BF16, "capped1_0"))
+        value_tiles(1, wv_high, sb("wv_codes1", [P, PASSES * HALF], U32))

@@ -186,23 +186,27 @@ def tile_list_mlat_cap_kernel(
                 weave(copy, rounded[:, a * PACK * HALF : (a + 1) * PACK * HALF], wv_raw[half, a][:])
             return rounded
 
-        def score_tiles(jh, mt0, capped):
-            count = capped.shape[1]
-            for i in range(count):
+        def cap_scores(jh, mt0, capped):
+            for i in range(capped.shape[1]):
                 bank = psum.tile([P, BANK], F32, name="bank_b")
                 product(bank, qa_mx[mt0 + i], jh)
                 nc.scalar.activation(capped[:, i, :], bank[:], TANH, bias=bias[:], scale=0.00390625)
-            score = sb("score%d_%d" % (jh, mt0), [P, count, BANK], F32)
+            return capped
+
+        def store_scores(jh, mt0, capped, score):
             nc.vector.tensor_scalar(score[:], capped[:], 8.0, None, MULT)
             nc.sync.dma_start(
-                out=out_0[mt0 * P : (mt0 + count) * P, jh * BANK : (jh + 1) * BANK].rearrange(
+                out=out_0[mt0 * P : (mt0 + capped.shape[1]) * P, jh * BANK : (jh + 1) * BANK].rearrange(
                     "(i p) c -> p i c", p=P
                 ),
                 in_=score[:],
             )
 
-        def value_tiles(half, rounded, codes):
-            wv_mx = quantise("wv%d" % half, rounded[:], codes)
+        def score_tiles(jh, mt0, capped):
+            cap_scores(jh, mt0, capped)
+            store_scores(jh, mt0, capped, sb("score%d_%d" % (jh, mt0), list(capped.shape), F32))
+
+        def value_tiles(half, wv_mx):
             for i in range(2):
                 nt = 2 * half + i
                 value = sb("value%d" % nt, [P, J], F32)
@@ -212,9 +216,9 @@ def tile_list_mlat_cap_kernel(
                     cols = slice(jh * BANK, (jh + 1) * BANK)
                     on_vector = half == 1 and jh == 1
                     (nc.vector.tensor_copy if on_vector else nc.scalar.copy)(out=value[:, cols], in_=bank[:])
-                    if nt == N // P - 1:
+                    if half == 1:
                         nc.sync.dma_start(out=out_1[nt * P : (nt + 1) * P, cols], in_=value[:, cols])
-                if nt < N // P - 1:
+                if half == 0:
                     nc.sync.dma_start(out=out_1[nt * P : (nt + 1) * P, :], in_=value[:])
 
         wv_low = round_wv(nc.scalar.copy, 0, sb("wv_low", [P, PASSES * PACK * HALF], BF16))
@@ -222,7 +226,9 @@ def tile_list_mlat_cap_kernel(
         score_tiles(0, 1, relayed("capped0_1", [P, 1, BANK], F32, 4160))
         score_tiles(0, 2, relayed("capped0_2", [P, 2, BANK], F32, 6208))
         score_tiles(1, 0, sb("capped1_0", [P, 2, BANK], F32))
-        score_tiles(1, 2, sb("capped1_2", [P, 2, BANK], F32))
-        value_tiles(0, wv_low, relayed("wv_codes0", [P, PASSES * HALF], U32, 8256))
-        wv_high = round_wv(nc.vector.tensor_copy, 1, sb("wv_high", [P, PASSES * PACK * HALF], BF16, "capped1_0"))
-        value_tiles(1, wv_high, sb("wv_codes1", [P, PASSES * HALF], U32))
+        capped_last = cap_scores(1, 2, sb("capped1_2", [P, 2, BANK], F32))
+        value_tiles(0, quantise("wv0", wv_low[:], relayed("wv_codes0", [P, PASSES * HALF], U32, 4160)))
+        wv_high = round_wv(nc.vector.tensor_copy, 1, relayed("wv_high", [P, PASSES * PACK * HALF], BF16, 6208))
+        wv_high_mx = quantise("wv1", wv_high[:], sb("wv_codes1", [P, PASSES * HALF], U32))
+        store_scores(1, 2, capped_last, relayed("score1_2", [P, 2, BANK], F32, 6208))
+        value_tiles(1, wv_high_mx)

@@ -186,25 +186,13 @@ def tile_list_mlat_cap_kernel(
                 weave(copy, rounded[:, a * PACK * HALF : (a + 1) * PACK * HALF], wv_raw[half, a][:])
             return rounded
 
-        def cap_scores(jh, mt0, capped):
-            for i in range(capped.shape[1]):
-                bank = psum.tile([P, BANK], F32, name="bank_b")
-                product(bank, qa_mx[mt0 + i], jh)
-                nc.scalar.activation(capped[:, i, :], bank[:], TANH, bias=bias[:], scale=0.00390625)
-            return capped
-
-        def store_scores(jh, mt0, capped, score):
-            nc.vector.tensor_scalar(score[:], capped[:], 8.0, None, MULT)
-            nc.sync.dma_start(
-                out=out_0[mt0 * P : (mt0 + capped.shape[1]) * P, jh * BANK : (jh + 1) * BANK].rearrange(
-                    "(i p) c -> p i c", p=P
-                ),
-                in_=score[:],
-            )
-
-        def score_tiles(jh, mt0, capped):
-            cap_scores(jh, mt0, capped)
-            store_scores(jh, mt0, capped, sb("score%d_%d" % (jh, mt0), list(capped.shape), F32))
+        def score_tile(jh, mt, capped):
+            bank = psum.tile([P, BANK], F32, name="bank_b")
+            product(bank, qa_mx[mt], jh)
+            nc.scalar.activation(capped, bank[:], TANH, bias=bias[:], scale=0.00390625)
+            score = sb("score%d_%d" % (jh, mt), [P, BANK], F32)
+            nc.vector.tensor_scalar(score[:], capped, 8.0, None, MULT)
+            nc.sync.dma_start(out=out_0[mt * P : (mt + 1) * P, jh * BANK : (jh + 1) * BANK], in_=score[:])
 
         def value_tiles(half, wv_mx):
             for i in range(2):
@@ -222,13 +210,13 @@ def tile_list_mlat_cap_kernel(
                     nc.sync.dma_start(out=out_1[nt * P : (nt + 1) * P, :], in_=value[:])
 
         wv_low = round_wv(nc.scalar.copy, 0, sb("wv_low", [P, PASSES * PACK * HALF], BF16))
-        score_tiles(0, 0, relayed("capped0_0", [P, 1, BANK], F32, 2112))
-        score_tiles(0, 1, relayed("capped0_1", [P, 1, BANK], F32, 4160))
-        score_tiles(0, 2, relayed("capped0_2", [P, 2, BANK], F32, 6208))
-        score_tiles(1, 0, sb("capped1_0", [P, 2, BANK], F32))
-        capped_last = cap_scores(1, 2, sb("capped1_2", [P, 2, BANK], F32))
-        value_tiles(0, quantise("wv0", wv_low[:], relayed("wv_codes0", [P, PASSES * HALF], U32, 4160)))
-        wv_high = round_wv(nc.vector.tensor_copy, 1, relayed("wv_high", [P, PASSES * PACK * HALF], BF16, 6208))
-        wv_high_mx = quantise("wv1", wv_high[:], sb("wv_codes1", [P, PASSES * HALF], U32))
-        store_scores(1, 2, capped_last, relayed("score1_2", [P, 2, BANK], F32, 6208))
-        value_tiles(1, wv_high_mx)
+        score_tile(0, 0, relayed("capped0_0", [P, BANK], F32, 2112)[:])
+        score_tile(0, 1, relayed("capped0_1", [P, BANK], F32, 4160)[:])
+        capped_pair = relayed("capped0_23", [P, 2 * BANK], F32, 6208)
+        score_tile(0, 2, capped_pair[:, :BANK])
+        score_tile(0, 3, capped_pair[:, BANK:])
+        for mt in range(M // P):
+            score_tile(1, mt, sb("capped1_%d" % mt, [P, BANK], F32)[:])
+        value_tiles(0, quantise("wv0", wv_low[:], relayed("wv_codes0", [P, PASSES * HALF], U32, 8256)))
+        wv_high = round_wv(nc.vector.tensor_copy, 1, sb("wv_high", [P, PASSES * PACK * HALF], BF16, "capped1_3"))
+        value_tiles(1, quantise("wv1", wv_high[:], sb("wv_codes1", [P, PASSES * HALF], U32)))

from contextlib import ExitStack

import concourse.mybir as mybir

K, R, M, T, N, J = 512, 1024, 512, 4096, 512, 1024
FLOPS = 2 * K * R * M + 2 * R * M * J + 2 * R * N * J

F32 = mybir.dt.float32
BF16 = mybir.dt.bfloat16
I32 = mybir.dt.int32
U32 = mybir.dt.uint32
U16 = mybir.dt.uint16
U8 = mybir.dt.uint8
FP8X4 = mybir.dt.float8_e4m3fn_x4
FP4X4 = mybir.dt.float4_e2m1fn_x4
TANH = mybir.ActivationFunctionType.Tanh
MULT = mybir.AluOpType.mult

P = 128
PACK = 4
PASSES = R // (P * PACK)
BANK = 512
HALF = 256


def tile_list_mlat_cap_kernel(
    tc, x, w4_words, w4_scales, tab_words, tab_scales, wv, offs, out_0, out_1
):
    nc = tc.nc
    with ExitStack() as ctx:
        keep = ctx.enter_context(tc.tile_pool(name="keep", bufs=1))
        relay = ctx.enter_context(tc.tile_pool(name="relay", bufs=1))
        psum = ctx.enter_context(tc.psum_pool(name="psum", bufs=4))

        def sb(name, shape, dtype, tag=None):
            return keep.tile(shape, dtype, name=name, tag=tag or name, align_bytes=64)

        def relayed(name, shape, dtype, offset):
            return relay.tile(shape, dtype, name=name, offset=offset, align_bytes=64)

        offsets = keep.tile([P, J // 16], U16, name="offsets")
        w4_raw = sb("w4_raw", [P, 2 * R], U8)
        w4s_raw = sb("w4s_raw", [P, R], U8)
        x_raw = sb("x_raw", [P, PACK, M], F32)
        tab_win = sb("tab_win", [P, T], U32)
        ts_win = sb("ts_win", [P, T], U8)
        wv_raw = {
            (0, 0): relayed("wv_raw00", [P, PACK, HALF], F32, 0),
            (0, 1): relayed("wv_raw01", [P, PACK, HALF], F32, 4096),
            (1, 0): sb("wv_raw10", [P, PACK, HALF], F32),
            (1, 1): sb("wv_raw11", [P, PACK, HALF], F32),
        }
        ts_plane = sb("ts_plane", [P, PASSES * J], U8)
        zero = sb("zero", [P, 1], F32)
        bias = sb("bias", [P, 1], F32)

        nc.vector.memset(w4s_raw[:].bitcast(I32), 0)
        nc.vector.memset(zero[:], 0.0)
        nc.vector.memset(ts_win[0:96, :].bitcast(I32), 0)
        nc.vector.memset(ts_plane[:].bitcast(I32), 0)

        nc.sync.dma_start(offsets[:], offs)
        nc.sync.dma_start(
            out=ts_win[96:P, :].bitcast(I32),
            in_=tab_scales.rearrange("a q t -> q a t").bitcast(I32),
        )
        nc.sync.dma_start(out=w4_raw[:].bitcast(I32), in_=w4_words[0].bitcast(I32))
        for quad in range(4):
            nc.sync.dma_start(
                out=w4s_raw[32 * quad : 32 * quad + 4, :].bitcast(I32),
                in_=w4_scales[0, 4 * quad : 4 * quad + 4, :].bitcast(I32),
            )
        nc.sync.dma_start(out=x_raw[:], in_=x.rearrange("(p j) m -> p j m", j=PACK))
        nc.sync.dma_start(
            out=tab_win[:].bitcast(I32), in_=tab_words[0].rearrange("p t b -> p (t b)").bitcast(I32)
        )
        nc.scalar.activation(bias[:], zero[:], TANH)

        ts_got = sb("ts_got", [P, J], U8)
        nc.vector.tensor_copy(ts_got[:], ts_win[:].indirect(offsets[:]))
        for quad in range(4):
            nc.sync.dma_start(
                out=ts_plane[32 * quad : 32 * quad + 4, :].bitcast(I32).rearrange("r (a w) -> r a w", a=PASSES),
                in_=ts_got[96 + 8 * quad : 96 + 8 * quad + 8, :].bitcast(I32),
            )
        for half in range(N // HALF):
            for a in range(PASSES):
                nc.sync.dma_start(
                    out=wv_raw[half, a][:],
                    in_=wv[a * P * PACK : (a + 1) * P * PACK, half * HALF : (half + 1) * HALF].rearrange(
                        "(p j) n -> p j n", j=PACK
                    ),
                )

        w4_ord = sb("w4_ord", [P, 2 * R], U8)
        w4s_ord = sb("w4s_ord", [P, R], U8)
        nc.vector.tensor_copy(
            out=w4_ord[:].bitcast(U16).rearrange("p (b t c i) -> p b c t i", b=PASSES, t=PACK, i=8),
            in_=w4_raw[:].bitcast(U16).rearrange("p (b c i t) -> p b c t i", b=PASSES, t=PACK, i=8),
        )
        nc.vector.tensor_copy(
            out=w4s_ord[:].rearrange("p (b t c i) -> p b c t i", b=PASSES, t=PACK, i=16),
            in_=w4s_raw[:].rearrange("p (b c i t) -> p b c t i", b=PASSES, t=PACK, i=16),
        )

        def weave(copy, dst, src):
            copy(
                out=dst.rearrange("p (c i t) -> p c t i", t=PACK, i=4),
                in_=src.rearrange("p t (c i) -> p c t i", i=4),
            )

        def quantise(name, rounded, codes):
            scales = sb(name + "_scales", [P, codes.shape[1]], U8)
            nc.vector.quantize_mx(out=codes[:].bitcast(FP8X4), scales=scales[:], in_=rounded)
            return [(codes[:, c0 : c0 + P], scales[:, c0 : c0 + P]) for c0 in range(0, codes.shape[1], P)]

        x_mx = []
        for group, tiles in enumerate(((0,), (1,), (2, 3))):
            x_bf = sb("x_bf%d" % group, [P, len(tiles) * BANK], BF16)
            for i, mt in enumerate(tiles):
                weave(nc.scalar.copy, x_bf[:, i * BANK : (i + 1) * BANK], x_raw[:, :, mt * P : (mt + 1) * P])
            x_mx.extend(quantise("x%d" % group, x_bf[:], sb("x_codes%d" % group, [P, len(tiles) * P], U32)))

        qa_mx = []

        def project(mt, qa_bf):
            for b in range(PASSES):
                bank = psum.tile([P, BANK], F32, name="bank_a")
                for t in range(PACK):
                    c0 = (b * PACK + t) * P
                    nc.tensor.matmul_mx(
                        out=bank[:, t * P : (t + 1) * P],
                        lhsT=w4_ord[:, 2 * c0 : 2 * (c0 + P)].bitcast(FP4X4),
                        lhsT_scale=w4s_ord[:, c0 : c0 + P],
                        rhs=x_mx[mt][0].bitcast(FP8X4),
                        rhs_scale=x_mx[mt][1],
                        start=True,
                        stop=True,
                    )
                (nc.vector.tensor_copy if mt == 0 else nc.scalar.copy)(
                    out=qa_bf[:, b * BANK : (b + 1) * BANK].rearrange("p (m t) -> p m t", t=PACK),
                    in_=bank[:].rearrange("p (t m) -> p m t", t=PACK),
                )

        def quantise_qa(pair, qa_bf):
            tiles = quantise("qa%d" % pair, qa_bf[:], sb("qa_codes%d" % pair, [P, 2 * PASSES * P], U32))
            qa_mx.extend([tiles[:PASSES], tiles[PASSES:]])

        def gather_words(jh):
            got = sb("tab_got%d" % jh, [P, BANK], U32, "tab_got")
            nc.vector.tensor_copy(got[:], tab_win[:].indirect(offsets[:, jh * 32 : (jh + 1) * 32]))
            return got

        def part_words(jh, got, pieces):
            parts = sb("tab_parts%d" % jh, [P, PASSES * 2 * BANK], U8)
            dst = parts[:].bitcast(U16).rearrange("p (a c i) -> p c a i", a=PASSES, i=8)
            src = got[:].bitcast(U16).rearrange("p (c i a) -> p c a i", a=PASSES, i=8)
            step = PASSES // pieces
            for a in range(0, PASSES, step):
                nc.vector.tensor_copy(out=dst[:, :, a : a + step, :], in_=src[:, :, a : a + step, :])
            return parts

        qa_rounded = [sb("qa_bf%d" % pair, [P, 2 * PASSES * BANK], BF16) for pair in range(2)]
        for mt in range(M // P):
            project(mt, qa_rounded[mt // 2][:, (mt % 2) * PASSES * BANK : (mt % 2 + 1) * PASSES * BANK])
            if mt == 1:
                quantise_qa(0, qa_rounded[0])
        tab_parts = [part_words(0, gather_words(0), 2)]
        quantise_qa(1, qa_rounded[1])
        tab_parts.append(part_words(1, gather_words(1), 1))

        def product(bank, operand, jh):
            for a, (codes, scales) in enumerate(operand):
                nc.tensor.matmul_mx(
                    out=bank[:],
                    lhsT=codes.bitcast(FP8X4),
                    lhsT_scale=scales,
                    rhs=tab_parts[jh][:, a * 2 * BANK : (a + 1) * 2 * BANK].bitcast(FP4X4),
                    rhs_scale=ts_plane[:, a * J + jh * BANK : a * J + (jh + 1) * BANK],
                    start=(a == 0),
                    stop=(a == PASSES - 1),
                )

        def round_wv(copy, half, rounded):
            for a in range(PASSES):
                weave(copy, rounded[:, a * PACK * HALF : (a + 1) * PACK * HALF], wv_raw[half, a][:])
            return rounded

        def score_tile(jh, mt, capped):
            bank = psum.tile([P, BANK], F32, name="bank_b")
            product(bank, qa_mx[mt], jh)
            nc.scalar.activation(capped, bank[:], TANH, bias=bias[:], scale=0.00390625)
            score = sb("score%d_%d" % (jh, mt), [P, BANK], F32)
            nc.vector.tensor_scalar(score[:], capped, 8.0, None, MULT)
            nc.sync.dma_start(out=out_0[mt * P : (mt + 1) * P, jh * BANK : (jh + 1) * BANK], in_=score[:])

        def value_tiles(half, wv_mx):
            for i in range(2):
                nt = 2 * half + i
                value = sb("value%d" % nt, [P, J], F32)
                for jh in range(J // BANK):
                    bank = psum.tile([P, BANK], F32, name="bank_a")
                    product(bank, [wv_mx[2 * a + i] for a in range(PASSES)], jh)
                    cols = slice(jh * BANK, (jh + 1) * BANK)
                    on_vector = half == 1 and jh == 1
                    (nc.vector.tensor_copy if on_vector else nc.scalar.copy)(out=value[:, cols], in_=bank[:])
                    if half == 1:
                        nc.sync.dma_start(out=out_1[nt * P : (nt + 1) * P, cols], in_=value[:, cols])
                if half == 0:
                    nc.sync.dma_start(out=out_1[nt * P : (nt + 1) * P, :], in_=value[:])

        wv_low = round_wv(nc.scalar.copy, 0, sb("wv_low", [P, PASSES * PACK * HALF], BF16))
        score_tile(0, 0, relayed("capped0_0", [P, BANK], F32, 2112)[:])
        score_tile(0, 1, relayed("capped0_1", [P, BANK], F32, 4160)[:])
        capped_pair = relayed("capped0_23", [P, 2 * BANK], F32, 6208)
        score_tile(0, 2, capped_pair[:, :BANK])
        score_tile(0, 3, capped_pair[:, BANK:])
        for mt in range(M // P):
            score_tile(1, mt, sb("capped1_%d" % mt, [P, BANK], F32)[:])
        value_tiles(0, quantise("wv0", wv_low[:], relayed("wv_codes0", [P, PASSES * HALF], U32, 8256)))
        wv_high = round_wv(nc.vector.tensor_copy, 1, sb("wv_high", [P, PASSES * PACK * HALF], BF16, "capped1_3"))
        value_tiles(1, quantise("wv1", wv_high[:], sb("wv_codes1", [P, PASSES * HALF], U32)))
